import numpy as np
import ml_dtypes


def mxq(x, axis, fmt="e4m3"):
    dtype, down = {"e4m3": (ml_dtypes.float8_e4m3fn, 7), "e5m2": (ml_dtypes.float8_e5m2, 14)}[fmt]
    v = np.moveaxis(np.asarray(x, np.float32).astype(ml_dtypes.bfloat16).astype(np.float64), axis, -1)
    blocks = v.reshape(v.shape[:-1] + (-1, 32))
    amax = np.abs(blocks).max(-1, keepdims=True)
    byte = np.maximum(np.where(amax > 0, np.frexp(amax)[1] - 1 + 127, 0) - down, 1)
    scale = np.exp2(byte - 127.0)
    codes = (blocks / scale).astype(np.float32).astype(dtype).astype(np.float64)
    return np.moveaxis((codes * scale).reshape(v.shape), -1, axis)


WIDE = False


def mx_kscale(k):
    if not WIDE:
        return np.ones(k)
    levels = np.array([10, -10, 5, -5, 0])
    if k % 512:
        return np.exp2(np.random.permutation(np.resize(levels, k // 32))).repeat(32)
    a = np.empty((k // 512, 16))
    for p in range(k // 512):
        a[p, :8] = np.random.permutation(np.resize(levels, 8))
        for g in range(8):
            far = levels[np.abs(levels - a[p, g]) >= 10]
            a[p, g + 8] = far[np.random.randint(len(far))]
    return np.exp2(a.ravel()).repeat(32)


def f64(x):
    return np.asarray(x).astype(np.float64)


def striped(idx):
    return np.tile(np.asarray(idx).reshape(-1, 16).T, (8, 1)).astype(np.uint16)


def unstriped(offs):
    return offs[:16].T.reshape(-1).astype(np.int64)


E2M1 = np.array([0.0, 0.5, 1.0, 1.5, 2.0, 3.0, 4.0, 6.0, -0.0, -0.5, -1.0, -1.5, -2.0, -3.0, -4.0, -6.0])


def pack_weight(w, fmt):
    k, n = w.shape
    w = f64(np.asarray(w, np.float32).astype(ml_dtypes.bfloat16)).reshape(k // 32, 32, n)
    amax = np.abs(w).max(1)
    if fmt == "e4m3":
        byte = np.frexp(amax)[1] - 1 + 127 - 7
    else:
        mant, ex = np.frexp(amax / 6.0)
        byte = np.where(mant > 0.5, ex, ex - 1) + 127
    byte = np.clip(np.where(amax > 0, byte, 1), 1, 254)
    scaled = (w * np.exp2(127.0 - byte)[:, None, :]).reshape(k, n).astype(np.float32)
    by_word = np.ascontiguousarray(scaled.reshape(k // 512, 128, 4, n).transpose(0, 1, 3, 2))
    if fmt == "e4m3":
        words = by_word.astype(ml_dtypes.float8_e4m3fn).view(np.uint8)
    else:
        c = by_word.astype(ml_dtypes.float4_e2m1fn).view(np.uint8) & 0xF
        words = (c[..., 0::2] | (c[..., 1::2] << 4)).reshape(k // 512, 128, 2 * n)
    return np.ascontiguousarray(words), np.ascontiguousarray(byte.astype(np.uint8).reshape(k // 512, 16, n))


def unpack_weight(words, scales, fmt):
    g, _, n = scales.shape
    words = np.ascontiguousarray(words).reshape(g, 128, n, -1)
    if fmt == "e4m3":
        vals = words.view(ml_dtypes.float8_e4m3fn).astype(np.float64)
    else:
        nib = np.empty((g, 128, n, 4), np.uint8)
        nib[..., 0::2] = words & 0xF
        nib[..., 1::2] = words >> 4
        vals = E2M1[nib]
    vals = vals * np.repeat(np.exp2(scales.astype(np.float64) - 127.0), 8, axis=1)[..., None]
    return vals.transpose(0, 1, 3, 2).reshape(g * 512, n)


def bf(x):
    return np.asarray(x, np.float32).astype(ml_dtypes.bfloat16)


def planes(Y):
    r, m = Y.shape
    b = f64(bf(Y)).reshape(r // 32, 32, m)
    amax = np.abs(b).max(1)
    byte = np.clip(np.where(amax > 0, np.frexp(amax)[1] - 1 + 127 - 7, 1), 1, 254)
    codes = (b * np.exp2(127.0 - byte)[:, None, :]).reshape(r, m).astype(np.float32).astype(ml_dtypes.float8_e4m3fn).view(np.uint8)
    words = codes.reshape(r // 512, 128, 4, m).transpose(0, 1, 3, 2)
    return np.ascontiguousarray(words), np.ascontiguousarray(byte.astype(np.uint8).reshape(r // 512, 16, m))


K, T, J, I, N = 1024, 1024, 512, 512, 512


def setup_inputs():
    n = np.random.standard_normal
    idx = np.random.permutation(T)[:J]
    idx2 = np.random.permutation(T)[:I]
    fk = mx_kscale(K)
    wap = pack_weight(n((K, N)) * 1 / np.sqrt(K) * fk[:, None], "e2m1")
    return {
        "xq": (n((K, T)) / fk[:, None]).astype(np.float32),
        "wa_words": wap[0],
        "wa_scales": wap[1],
        "xr": (1.0 * n((N, T))).astype(np.float32),
        "gb": (np.random.uniform(0.5, 2.0, (1, I))).astype(np.float32),
        "ko": (np.random.uniform(-0.5, 0.5, (N, 1))).astype(np.float32),
        "offs": striped(idx),
        "offs2": striped(idx2),
    }


def reference(xq, wa_words, wa_scales, xr, gb, ko, offs, offs2):
    idx = unstriped(offs)
    idx2 = unstriped(offs2)
    wau = unpack_weight(wa_words, wa_scales, "e2m1")
    xqidxq = mxq(f64(xq)[:, idx], 0, "e4m3")
    p = wau.T @ xqidxq
    pg = np.zeros((N, T))
    pg[:, idx] = p
    d = f64(xr)[:, idx2] * f64(gb) + f64(ko)
    dp = np.zeros((N, T))
    dp[:, idx2] = d
    y = pg + 0.5 * dp
    words, scales = planes(y)
    return y, words, scales

@@ -1,0 +1,175 @@
+from contextlib import ExitStack
+
+import concourse.mybir as mybir
+from concourse.masks import make_identity
+
+K, T, J, N = 1024, 1024, 512, 512
+FLOPS = 2 * K * J * N
+
+F32 = mybir.dt.float32
+BF16 = mybir.dt.bfloat16
+I32 = mybir.dt.int32
+U32 = mybir.dt.uint32
+U16 = mybir.dt.uint16
+U8 = mybir.dt.uint8
+FP8X4 = mybir.dt.float8_e4m3fn_x4
+FP4X4 = mybir.dt.float4_e2m1fn_x4
+MULT = mybir.AluOpType.mult
+ADD = mybir.AluOpType.add
+COPY = mybir.ActivationFunctionType.Copy
+IDENT = mybir.ActivationFunctionType.Identity
+
+P = 128
+PACK = 4
+PASSES = K // (P * PACK)
+HALF = T // 2
+
+
+def tile_list_copying_expert_pl_kernel(tc, xq, wa_words, wa_scales, xr, gb, ko, offs, offs2, out_0, out_1, out_2):
+    nc = tc.nc
+    with ExitStack() as ctx:
+        lists = ctx.enter_context(tc.tile_pool(name="lists", bufs=1))
+        sb = ctx.enter_context(tc.tile_pool(name="sb", bufs=1))
+        ps = ctx.enter_context(tc.psum_pool(name="ps", bufs=1))
+
+        idx = lists.tile([P, J // 16], U16, name="idx")
+        idx2 = lists.tile([P, J // 16], U16, name="idx2")
+        gb_col = sb.tile([P, PACK], F32, name="gb_col", tag="pairs0", align_bytes=64)
+        ko_col = sb.tile([P, PACK], F32, name="ko_col")
+        xr_sb = [sb.tile([P, T], F32, name="xr%d" % t) for t in range(PACK)]
+        raw = [sb.tile([P, 2, T], F32, name="raw%d" % i, tag="raw%d" % i, align_bytes=64) for i in range(2 * PASSES)]
+        w_words = sb.tile([P, PASSES, 2 * N], U8, name="w_words", align_bytes=64)
+        w_scales = sb.tile([P, PASSES, N], U8, name="w_scales", align_bytes=64)
+        ident = sb.tile([P, P], F32, name="ident")
+        d_page = [sb.tile([P, T], F32, name="d_page%d" % i) for i in range(3)]
+        p_page = [sb.tile([P, T], F32, name="p_page%d" % i) for i in range(2)]
+
+        xr_rows = xr.rearrange("(p t) c -> p t c", t=PACK)
+        xq_rows = xq.rearrange("(a p u e) c -> a u p e c", a=PASSES, u=2, e=2)
+        y_rows = out_0.rearrange("(p t) c -> p t c", t=PACK)
+
+        nc.scalar.dma_start(gb_col[:], gb.rearrange("o (p m) -> p (o m)", m=PACK))
+        nc.scalar.dma_start(ko_col[:], ko.rearrange("(p t) o -> p (t o)", t=PACK))
+        nc.sync.dma_start(idx2[:], offs2)
+        nc.sync.dma_start(xr_sb[0][:], xr_rows[:, 0, :])
+        nc.sync.dma_start(raw[0][:], xq_rows[0, 0])
+        nc.sync.dma_start(xr_sb[1][:], xr_rows[:, 1, :])
+        nc.sync.dma_start(idx[:], offs)
+        nc.sync.dma_start(raw[1][:], xq_rows[0, 1])
+        nc.sync.dma_start(raw[2][:], xq_rows[1, 0])
+        nc.sync.dma_start(raw[3][:], xq_rows[1, 1])
+        nc.sync.dma_start(xr_sb[2][:], xr_rows[:, 2, :])
+        nc.sync.dma_start(xr_sb[3][:], xr_rows[:, 3, :])
+        nc.sync.dma_start(w_words[:].bitcast(I32), wa_words.rearrange("a p c -> p a c").bitcast(I32))
+
+        make_identity(nc, ident[:])
+        for page in (d_page[0], d_page[1]):
+            nc.vector.memset(page[:], 0.0)
+        nc.gpsimd.memset(w_scales[:].bitcast(I32), 0)
+        for page in (d_page[2], p_page[0], p_page[1]):
+            nc.gpsimd.memset(page[:], 0.0)
+        for q in range(4):
+            nc.sync.dma_start(
+                w_scales[32 * q : 32 * q + 4, :, :].bitcast(I32),
+                wa_scales[:, 4 * q : 4 * q + 4, :].rearrange("a r c -> r a c").bitcast(I32),
+            )
+
+        gb_ps = ps.tile([P, PACK, P], F32, name="gb_ps", tag="turn0")
+        for m in range(PACK):
+            nc.tensor.transpose(gb_ps[:, m, :], gb_col[:, m : m + 1].to_broadcast([P, P]), ident[:])
+        gb_half = sb.tile([P, J], F32, name="gb_half")
+        nc.scalar.activation(
+            gb_half[:].rearrange("p (n m) -> p n m", m=PACK), gb_ps[:].rearrange("p m n -> p n m"), COPY, scale=0.5
+        )
+        ko_half = sb.tile([P, PACK], F32, name="ko_half")
+        nc.scalar.activation(ko_half[:], ko_col[:], COPY, scale=0.5)
+        ko_wide = [sb.tile([P, J], F32, name="ko_wide%d" % t) for t in range(2)]
+        for t in range(2):
+            nc.scalar.activation(ko_wide[t][:], ko_col[:, t : t + 1].to_broadcast([P, J]), COPY, scale=0.5)
+
+        def gather_xr(t, tag):
+            picked = sb.tile([P, J], F32, name="picked%d" % t, tag=tag, align_bytes=64)
+            nc.vector.tensor_tensor(picked[:], xr_sb[t][:].indirect(idx2[:]), gb_half[:], MULT)
+            return picked
+
+        for t in range(2):
+            picked = gather_xr(t, "picked%d" % t)
+            nc.vector.tensor_tensor(d_page[t][:].indirect(idx2[:]), picked[:], ko_wide[t][:], ADD)
+
+        pairs = [sb.tile([P, T, 2], BF16, name="pairs%d" % i, tag="pairs%d" % i, align_bytes=64) for i in range(2 * PASSES)]
+        words = [sb.tile([P, 2, J], U32, name="words%d" % a, tag="words%d" % a) for a in range(PASSES)]
+        for i in range(2 * PASSES):
+            nc.scalar.activation(pairs[i][:], raw[i][:].rearrange("p e c -> p c e"), COPY)
+            window = pairs[i][:].rearrange("p c e -> p (c e)").bitcast(U32)
+            nc.vector.tensor_copy(words[i // 2][:, i % 2, :], window.indirect(idx[:]))
+
+        x_codes = [sb.tile([P, J], U32, name="x_codes%d" % a, align_bytes=64) for a in range(PASSES)]
+        x_scales = [sb.tile([P, J], U8, name="x_scales%d" % a, align_bytes=64) for a in range(PASSES)]
+        for a in range(PASSES):
+            woven = sb.tile([P, J * PACK], BF16, name="woven%d" % a, tag="raw%d" % (3 - a), align_bytes=64)
+            nc.scalar.copy(woven[:].bitcast(U32).rearrange("p (j u) -> p j u", u=2), words[a][:].rearrange("p u j -> p j u"))
+            nc.vector.quantize_mx(out=x_codes[a][:].bitcast(FP8X4), scales=x_scales[a][:], in_=woven[:])
+            if a == 0:
+                picked2 = gather_xr(2, "pairs3")
+
+        d_late = sb.tile([P, 2, J], F32, name="d_late", tag="words1")
+        nc.scalar.activation(d_late[:, 0, :], picked2[:], IDENT, bias=ko_half[:, 2:3], scale=1.0)
+        nc.vector.tensor_copy(d_page[2][:].indirect(idx2[:]), d_late[:, 0, :])
+
+        picked3 = gather_xr(3, "raw2")
+
+        acc = [ps.tile([P, N], F32, name="acc%d" % b) for b in range(J // P)]
+        for a in range(PASSES):
+            for b in range(J // P):
+                cols = slice(b * P, (b + 1) * P)
+                nc.tensor.matmul_mx(
+                    out=acc[b][:],
+                    lhsT=x_codes[a][:, cols].bitcast(FP8X4),
+                    lhsT_scale=x_scales[a][:, cols],
+                    rhs=w_words[:, a, :].bitcast(FP4X4),
+                    rhs_scale=w_scales[:, a, :],
+                    start=(a == 0),
+                    stop=(a == PASSES - 1),
+                )
+        p_t = [sb.tile([P, PACK, P], F32, name="p_t%d" % b) for b in range(J // P)]
+        for b in range(J // P):
+            nc.scalar.copy(p_t[b][:], acc[b][:].rearrange("p (q t) -> p t q", t=PACK))
+        p_sb = [sb.tile([P, J], F32, name="p_sb%d" % t) for t in range(PACK)]
+        for t in range(PACK):
+            turn = ps.tile([P, J], F32, name="turn%d" % t, tag="turn%d" % t)
+            for b in range(J // P):
+                nc.tensor.transpose(turn[:, b * P : (b + 1) * P], p_t[b][:, t, :], ident[:])
+            nc.scalar.copy(p_sb[t][:], turn[:])
+        nc.scalar.activation(d_late[:, 1, :], picked3[:], IDENT, bias=ko_half[:, 3:4], scale=1.0)
+
+        y = [[sb.tile([P, 2, HALF], F32, name="y%d_%d" % (u, h)) for h in range(2)] for u in range(2)]
+        y_bf = [sb.tile([P, HALF, PACK], BF16, name="y_bf%d" % h, align_bytes=64) for h in range(2)]
+        y_codes = [sb.tile([P, HALF], U32, name="y_codes%d" % h, align_bytes=64) for h in range(2)]
+        y_scales = sb.tile([P, T], U8, name="y_scales", align_bytes=64)
+        codes_out = out_1[0].rearrange("p c r -> p (c r)").bitcast(I32)
+
+        def add_and_store(engine, t, p_src, d_src):
+            for h in range(2):
+                cols = slice(h * HALF, (h + 1) * HALF)
+                engine.tensor_tensor(y[t // 2][h][:, t % 2, :], p_src[:, cols], d_src[:, cols], ADD)
+                nc.sync.dma_start(y_rows[:, t, cols], y[t // 2][h][:, t % 2, :])
+
+        for t in range(3):
+            nc.vector.tensor_copy(p_page[t % 2][:].indirect(idx[:]), p_sb[t][:])
+            add_and_store(nc.gpsimd, t, p_page[t % 2], d_page[t])
+        for h in range(2):
+            nc.scalar.activation(y_bf[h][:, :, 0:2], y[0][h][:].rearrange("p e c -> p c e"), COPY)
+        nc.vector.tensor_copy(d_page[1][:].indirect(idx2[:]), d_late[:, 1, :])
+        nc.vector.tensor_copy(p_page[1][:].indirect(idx[:]), p_sb[3][:])
+        add_and_store(nc.vector, 3, p_page[1], d_page[1])
+        nc.scalar.activation(y_bf[0][:, :, 2:4], y[1][0][:].rearrange("p e c -> p c e"), COPY)
+        nc.vector.tensor_copy(y_bf[1][:, :, 2:4], y[1][1][:].rearrange("p e c -> p c e"))
+        for h in (1, 0):
+            cols = slice(h * HALF, (h + 1) * HALF)
+            nc.vector.quantize_mx(
+                out=y_codes[h][:].bitcast(FP8X4), scales=y_scales[:, cols], in_=y_bf[h][:].rearrange("p c t -> p (c t)")
+            )
+            nc.sync.dma_start(codes_out[:, cols], y_codes[h][:].bitcast(I32))
+        for q in range(4):
+            queue = nc.scalar if q % 2 else nc.sync
+            queue.dma_start(out_2[0, 4 * q : 4 * q + 4, :].bitcast(I32), y_scales[32 * q : 32 * q + 4, :].bitcast(I32))

@@ -34,14 +34,14 @@ def tile_list_copying_expert_pl_kernel(tc, xq, wa_words, wa_scales, xr, gb, ko, 
 
         idx = lists.tile([P, J // 16], U16, name="idx")
         idx2 = lists.tile([P, J // 16], U16, name="idx2")
-        gb_col = sb.tile([P, PACK], F32, name="gb_col", tag="pairs0", align_bytes=64)
-        ko_col = sb.tile([P, PACK], F32, name="ko_col")
+        gb_col = sb.tile([P, PACK], F32, name="gb_col")
+        ko_col = sb.tile([P, PACK], F32, name="ko_col", tag="cast0", align_bytes=64)
         xr_sb = [sb.tile([P, T], F32, name="xr%d" % t) for t in range(PACK)]
         raw = [sb.tile([P, 2, T], F32, name="raw%d" % i, tag="raw%d" % i, align_bytes=64) for i in range(2 * PASSES)]
         w_words = sb.tile([P, PASSES, 2 * N], U8, name="w_words", align_bytes=64)
         w_scales = sb.tile([P, PASSES, N], U8, name="w_scales", align_bytes=64)
         ident = sb.tile([P, P], F32, name="ident")
-        d_page = [sb.tile([P, T], F32, name="d_page%d" % i) for i in range(3)]
+        d_page = [sb.tile([P, T], F32, name="d_page%d" % i) for i in range(PACK)]
         p_page = [sb.tile([P, T], F32, name="p_page%d" % i) for i in range(2)]
 
         xr_rows = xr.rearrange("(p t) c -> p t c", t=PACK)
@@ -52,21 +52,21 @@ def tile_list_copying_expert_pl_kernel(tc, xq, wa_words, wa_scales, xr, gb, ko, 
         nc.scalar.dma_start(ko_col[:], ko.rearrange("(p t) o -> p (t o)", t=PACK))
         nc.sync.dma_start(idx2[:], offs2)
         nc.sync.dma_start(xr_sb[0][:], xr_rows[:, 0, :])
+        nc.sync.dma_start(idx[:], offs)
         nc.sync.dma_start(raw[0][:], xq_rows[0, 0])
         nc.sync.dma_start(xr_sb[1][:], xr_rows[:, 1, :])
-        nc.sync.dma_start(idx[:], offs)
         nc.sync.dma_start(raw[1][:], xq_rows[0, 1])
+        nc.sync.dma_start(xr_sb[2][:], xr_rows[:, 2, :])
         nc.sync.dma_start(raw[2][:], xq_rows[1, 0])
         nc.sync.dma_start(raw[3][:], xq_rows[1, 1])
-        nc.sync.dma_start(xr_sb[2][:], xr_rows[:, 2, :])
-        nc.sync.dma_start(xr_sb[3][:], xr_rows[:, 3, :])
         nc.sync.dma_start(w_words[:].bitcast(I32), wa_words.rearrange("a p c -> p a c").bitcast(I32))
+        nc.sync.dma_start(xr_sb[3][:], xr_rows[:, 3, :])
 
         make_identity(nc, ident[:])
-        for page in (d_page[0], d_page[1]):
+        for page in d_page[:2]:
             nc.vector.memset(page[:], 0.0)
         nc.gpsimd.memset(w_scales[:].bitcast(I32), 0)
-        for page in (d_page[2], p_page[0], p_page[1]):
+        for page in d_page[2:] + p_page:
             nc.gpsimd.memset(page[:], 0.0)
         for q in range(4):
             nc.sync.dma_start(
@@ -78,98 +78,137 @@ def tile_list_copying_expert_pl_kernel(tc, xq, wa_words, wa_scales, xr, gb, ko, 
         for m in range(PACK):
             nc.tensor.transpose(gb_ps[:, m, :], gb_col[:, m : m + 1].to_broadcast([P, P]), ident[:])
         gb_half = sb.tile([P, J], F32, name="gb_half")
-        nc.scalar.activation(
-            gb_half[:].rearrange("p (n m) -> p n m", m=PACK), gb_ps[:].rearrange("p m n -> p n m"), COPY, scale=0.5
+        nc.vector.tensor_scalar(
+            gb_half[:].rearrange("p (n m) -> p n m", m=PACK), gb_ps[:].rearrange("p m n -> p n m"), 0.5, None, MULT
         )
         ko_half = sb.tile([P, PACK], F32, name="ko_half")
         nc.scalar.activation(ko_half[:], ko_col[:], COPY, scale=0.5)
-        ko_wide = [sb.tile([P, J], F32, name="ko_wide%d" % t) for t in range(2)]
-        for t in range(2):
-            nc.scalar.activation(ko_wide[t][:], ko_col[:, t : t + 1].to_broadcast([P, J]), COPY, scale=0.5)
+
+        def spread_ko(t, tag):
+            wide = sb.tile([P, J], F32, name="ko_wide%d" % t, tag=tag, align_bytes=64)
+            nc.scalar.copy(wide[:], ko_half[:, t : t + 1].to_broadcast([P, J]))
+            return wide
 
         def gather_xr(t, tag):
             picked = sb.tile([P, J], F32, name="picked%d" % t, tag=tag, align_bytes=64)
             nc.vector.tensor_tensor(picked[:], xr_sb[t][:].indirect(idx2[:]), gb_half[:], MULT)
             return picked
 
-        for t in range(2):
-            picked = gather_xr(t, "picked%d" % t)
-            nc.vector.tensor_tensor(d_page[t][:].indirect(idx2[:]), picked[:], ko_wide[t][:], ADD)
+        def scatter_d(t, picked, wide):
+            nc.vector.tensor_tensor(d_page[t][:].indirect(idx2[:]), picked[:], wide[:], ADD)
 
-        pairs = [sb.tile([P, T, 2], BF16, name="pairs%d" % i, tag="pairs%d" % i, align_bytes=64) for i in range(2 * PASSES)]
-        words = [sb.tile([P, 2, J], U32, name="words%d" % a, tag="words%d" % a) for a in range(PASSES)]
-        for i in range(2 * PASSES):
-            nc.scalar.activation(pairs[i][:], raw[i][:].rearrange("p e c -> p c e"), COPY)
-            window = pairs[i][:].rearrange("p c e -> p (c e)").bitcast(U32)
+        ko_wide = [spread_ko(t, "ko_wide%d" % t) for t in range(PACK)]
+        for t in range(3):
+            scatter_d(t, gather_xr(t, "picked%d" % t), ko_wide[t])
+
+        words = [sb.tile([P, 2, J], U32, name="words%d" % a, tag="words%d" % a, align_bytes=64) for a in range(PASSES)]
+        planes = sb.tile([P, 2, T], BF16, name="planes", tag="cast0", align_bytes=64)
+        nc.scalar.activation(planes[:], raw[0][:], COPY)
+        first = words[0][:, 0, :].bitcast(BF16).rearrange("p (j e) -> p j e", e=2)
+        for e in range(2):
+            nc.scalar.activation(first[:, :, e], planes[:, e, :].indirect(idx[:]), COPY)
+        for i in range(1, 2 * PASSES):
+            pairs = sb.tile([P, T, 2], BF16, name="pairs%d" % i, tag="cast%d" % i, align_bytes=64)
+            nc.scalar.activation(pairs[:], raw[i][:].rearrange("p e c -> p c e"), COPY)
+            window = pairs[:].rearrange("p c e -> p (c e)").bitcast(U32)
             nc.vector.tensor_copy(words[i // 2][:, i % 2, :], window.indirect(idx[:]))
 
-        x_codes = [sb.tile([P, J], U32, name="x_codes%d" % a, align_bytes=64) for a in range(PASSES)]
-        x_scales = [sb.tile([P, J], U8, name="x_scales%d" % a, align_bytes=64) for a in range(PASSES)]
-        for a in range(PASSES):
-            woven = sb.tile([P, J * PACK], BF16, name="woven%d" % a, tag="raw%d" % (3 - a), align_bytes=64)
-            nc.scalar.copy(woven[:].bitcast(U32).rearrange("p (j u) -> p j u", u=2), words[a][:].rearrange("p u j -> p j u"))
-            nc.vector.quantize_mx(out=x_codes[a][:].bitcast(FP8X4), scales=x_scales[a][:], in_=woven[:])
-            if a == 0:
-                picked2 = gather_xr(2, "pairs3")
+        x_codes = {}
+        x_scales = {}
 
-        d_late = sb.tile([P, 2, J], F32, name="d_late", tag="words1")
-        nc.scalar.activation(d_late[:, 0, :], picked2[:], IDENT, bias=ko_half[:, 2:3], scale=1.0)
-        nc.vector.tensor_copy(d_page[2][:].indirect(idx2[:]), d_late[:, 0, :])
+        def quantise_x(a, first_block, blocks, tag):
+            width = blocks * P
+            entries = slice(first_block * P, first_block * P + width)
+            woven = sb.tile([P, width * PACK], BF16, name="woven%d_%d" % (a, first_block), tag=tag, align_bytes=64)
+            codes = sb.tile([P, width], U32, name="x_codes%d_%d" % (a, first_block), align_bytes=64)
+            scales = sb.tile([P, width], U8, name="x_scales%d_%d" % (a, first_block), align_bytes=64)
+            nc.scalar.copy(
+                woven[:].bitcast(U32).rearrange("p (j u) -> p j u", u=2), words[a][:, :, entries].rearrange("p u j -> p j u")
+            )
+            nc.vector.quantize_mx(out=codes[:].bitcast(FP8X4), scales=scales[:], in_=woven[:])
+            for b in range(blocks):
+                x_codes[a, first_block + b] = codes[:, b * P : (b + 1) * P]
+                x_scales[a, first_block + b] = scales[:, b * P : (b + 1) * P]
 
-        picked3 = gather_xr(3, "raw2")
+        quantise_x(0, 0, 4, "raw3")
+        quantise_x(1, 0, 2, "woven_a")
+        quantise_x(1, 2, 2, "woven_b")
+        scatter_d(3, gather_xr(3, "woven_b"), ko_wide[3])
 
         acc = [ps.tile([P, N], F32, name="acc%d" % b) for b in range(J // P)]
         for a in range(PASSES):
             for b in range(J // P):
-                cols = slice(b * P, (b + 1) * P)
                 nc.tensor.matmul_mx(
                     out=acc[b][:],
-                    lhsT=x_codes[a][:, cols].bitcast(FP8X4),
-                    lhsT_scale=x_scales[a][:, cols],
+                    lhsT=x_codes[a, b].bitcast(FP8X4),
+                    lhsT_scale=x_scales[a, b],
                     rhs=w_words[:, a, :].bitcast(FP4X4),
                     rhs_scale=w_scales[:, a, :],
                     start=(a == 0),
                     stop=(a == PASSES - 1),
                 )
         p_t = [sb.tile([P, PACK, P], F32, name="p_t%d" % b) for b in range(J // P)]
-        for b in range(J // P):
-            nc.scalar.copy(p_t[b][:], acc[b][:].rearrange("p (q t) -> p t q", t=PACK))
-        p_sb = [sb.tile([P, J], F32, name="p_sb%d" % t) for t in range(PACK)]
-        for t in range(PACK):
-            turn = ps.tile([P, J], F32, name="turn%d" % t, tag="turn%d" % t)
-            for b in range(J // P):
-                nc.tensor.transpose(turn[:, b * P : (b + 1) * P], p_t[b][:, t, :], ident[:])
-            nc.scalar.copy(p_sb[t][:], turn[:])
-        nc.scalar.activation(d_late[:, 1, :], picked3[:], IDENT, bias=ko_half[:, 3:4], scale=1.0)
 
-        y = [[sb.tile([P, 2, HALF], F32, name="y%d_%d" % (u, h)) for h in range(2)] for u in range(2)]
-        y_bf = [sb.tile([P, HALF, PACK], BF16, name="y_bf%d" % h, align_bytes=64) for h in range(2)]
-        y_codes = [sb.tile([P, HALF], U32, name="y_codes%d" % h, align_bytes=64) for h in range(2)]
+        def leave_bank(b):
+            nc.scalar.copy(p_t[b][:], acc[b][:].rearrange("p (q t) -> p t q", t=PACK))
+
+        def turn_p(t, blocks, bank):
+            width = len(blocks) * P
+            turn = ps.tile([P, width], F32, name="turn%d_%d" % (t, blocks[0]), tag="turn%d" % bank)
+            for i, b in enumerate(blocks):
+                nc.tensor.transpose(turn[:, i * P : (i + 1) * P], p_t[b][:, t, :], ident[:])
+            p_sb = sb.tile([P, width], F32, name="p_sb%d_%d" % (t, blocks[0]))
+            nc.scalar.copy(p_sb[:], turn[:])
+            return p_sb
+
+        def scatter_p(t, blocks, p_sb):
+            entries = idx[:, blocks[0] * (P // 16) : (blocks[-1] + 1) * (P // 16)]
+            nc.vector.tensor_copy(p_page[t % 2][:].indirect(entries), p_sb[:])
+
+        leave_bank(0)
+        leave_bank(1)
+        scatter_p(0, [0, 1], turn_p(0, [0, 1], 0))
+        leave_bank(2)
+        leave_bank(3)
+        scatter_p(0, [2, 3], turn_p(0, [2, 3], 1))
+        p_rest = [turn_p(t, [0, 1, 2, 3], (t + 1) % 4) for t in range(1, PACK)]
+
+        pieces = [slice(0, T // 4), slice(T // 4, 3 * T // 4), slice(3 * T // 4, T)]
+        y_low = sb.tile([P, 2, T], F32, name="y_low")
+        y_high = [sb.tile([P, 2, c.stop - c.start], F32, name="y_high%d" % i) for i, c in enumerate(pieces)]
+        y_bf = [sb.tile([P, c.stop - c.start, PACK], BF16, name="y_bf%d" % i, align_bytes=64) for i, c in enumerate(pieces)]
+        y_codes = sb.tile([P, T], U32, name="y_codes", align_bytes=64)
         y_scales = sb.tile([P, T], U8, name="y_scales", align_bytes=64)
         codes_out = out_1[0].rearrange("p c r -> p (c r)").bitcast(I32)
 
-        def add_and_store(engine, t, p_src, d_src):
-            for h in range(2):
-                cols = slice(h * HALF, (h + 1) * HALF)
-                engine.tensor_tensor(y[t // 2][h][:, t % 2, :], p_src[:, cols], d_src[:, cols], ADD)
-                nc.sync.dma_start(y_rows[:, t, cols], y[t // 2][h][:, t % 2, :])
+        def add_low(t):
+            nc.gpsimd.tensor_tensor(y_low[:, t, :], p_page[t][:], d_page[t][:], ADD)
+            nc.sync.dma_start(y_rows[:, t, :], y_low[:, t, :])
 
-        for t in range(3):
-            nc.vector.tensor_copy(p_page[t % 2][:].indirect(idx[:]), p_sb[t][:])
-            add_and_store(nc.gpsimd, t, p_page[t % 2], d_page[t])
-        for h in range(2):
-            nc.scalar.activation(y_bf[h][:, :, 0:2], y[0][h][:].rearrange("p e c -> p c e"), COPY)
-        nc.vector.tensor_copy(d_page[1][:].indirect(idx2[:]), d_late[:, 1, :])
-        nc.vector.tensor_copy(p_page[1][:].indirect(idx[:]), p_sb[3][:])
-        add_and_store(nc.vector, 3, p_page[1], d_page[1])
-        nc.scalar.activation(y_bf[0][:, :, 2:4], y[1][0][:].rearrange("p e c -> p c e"), COPY)
-        nc.vector.tensor_copy(y_bf[1][:, :, 2:4], y[1][1][:].rearrange("p e c -> p c e"))
-        for h in (1, 0):
-            cols = slice(h * HALF, (h + 1) * HALF)
+        def add_high(engine, t):
+            for i, cols in enumerate(pieces):
+                engine.tensor_tensor(y_high[i][:, t - 2, :], p_page[t - 2][:, cols], d_page[t][:, cols], ADD)
+                nc.sync.dma_start(y_rows[:, t, cols], y_high[i][:, t - 2, :])
+
+        add_low(0)
+        scatter_p(1, [0, 1, 2, 3], p_rest[0])
+        add_low(1)
+        scatter_p(2, [0, 1, 2, 3], p_rest[1])
+        for i, cols in enumerate(pieces):
+            nc.scalar.activation(y_bf[i][:, :, 0:2], y_low[:, :, cols].rearrange("p e c -> p c e"), COPY)
+        add_high(nc.gpsimd, 2)
+        scatter_p(3, [0, 1, 2, 3], p_rest[2])
+        add_high(nc.vector, 3)
+        for i in (0, 2):
+            nc.scalar.activation(y_bf[i][:, :, 2:4], y_high[i][:].rearrange("p e c -> p c e"), COPY)
+        nc.vector.tensor_copy(y_bf[1][:, :, 2:4], y_high[1][:].rearrange("p e c -> p c e"))
+        for i, cols in enumerate(pieces):
             nc.vector.quantize_mx(
-                out=y_codes[h][:].bitcast(FP8X4), scales=y_scales[:, cols], in_=y_bf[h][:].rearrange("p c t -> p (c t)")
+                out=y_codes[:, cols].bitcast(FP8X4), scales=y_scales[:, cols], in_=y_bf[i][:].rearrange("p c t -> p (c t)")
             )
-            nc.sync.dma_start(codes_out[:, cols], y_codes[h][:].bitcast(I32))
+            if i > 0:
+                done = slice(0, cols.stop) if i == 1 else cols
+                nc.sync.dma_start(codes_out[:, done], y_codes[:, done].bitcast(I32))
         for q in range(4):
-            queue = nc.scalar if q % 2 else nc.sync
+            queue = nc.scalar if q % 2 == 0 else nc.sync
             queue.dma_start(out_2[0, 4 * q : 4 * q + 4, :].bitcast(I32), y_scales[32 * q : 32 * q + 4, :].bitcast(I32))

@@ -53,12 +53,13 @@ def tile_list_copying_expert_pl_kernel(tc, xq, wa_words, wa_scales, xr, gb, ko, 
         nc.sync.dma_start(idx2[:], offs2)
         nc.sync.dma_start(xr_sb[0][:], xr_rows[:, 0, :])
         nc.sync.dma_start(idx[:], offs)
-        nc.sync.dma_start(raw[0][:], xq_rows[0, 0])
+        for e in range(2):
+            nc.sync.dma_start(raw[0][:, e, :], xq_rows[0, 0][:, e, :])
         nc.sync.dma_start(xr_sb[1][:], xr_rows[:, 1, :])
-        nc.sync.dma_start(raw[1][:], xq_rows[0, 1])
-        nc.sync.dma_start(xr_sb[2][:], xr_rows[:, 2, :])
         nc.sync.dma_start(raw[2][:], xq_rows[1, 0])
         nc.sync.dma_start(raw[3][:], xq_rows[1, 1])
+        nc.sync.dma_start(raw[1][:], xq_rows[0, 1])
+        nc.sync.dma_start(xr_sb[2][:], xr_rows[:, 2, :])
         nc.sync.dma_start(w_words[:].bitcast(I32), wa_words.rearrange("a p c -> p a c").bitcast(I32))
         nc.sync.dma_start(xr_sb[3][:], xr_rows[:, 3, :])
 
@@ -81,72 +82,70 @@ def tile_list_copying_expert_pl_kernel(tc, xq, wa_words, wa_scales, xr, gb, ko, 
         nc.vector.tensor_scalar(
             gb_half[:].rearrange("p (n m) -> p n m", m=PACK), gb_ps[:].rearrange("p m n -> p n m"), 0.5, None, MULT
         )
-        ko_half = sb.tile([P, PACK], F32, name="ko_half")
-        nc.scalar.activation(ko_half[:], ko_col[:], COPY, scale=0.5)
-
-        def spread_ko(t, tag):
-            wide = sb.tile([P, J], F32, name="ko_wide%d" % t, tag=tag, align_bytes=64)
-            nc.scalar.copy(wide[:], ko_half[:, t : t + 1].to_broadcast([P, J]))
-            return wide
+        ko_wide = sb.tile([P, PACK, J], F32, name="ko_wide")
+        nc.scalar.activation(ko_wide[:], ko_col[:].unsqueeze(2).to_broadcast([P, PACK, J]), COPY, scale=0.5)
 
         def gather_xr(t, tag):
             picked = sb.tile([P, J], F32, name="picked%d" % t, tag=tag, align_bytes=64)
             nc.vector.tensor_tensor(picked[:], xr_sb[t][:].indirect(idx2[:]), gb_half[:], MULT)
             return picked
 
-        def scatter_d(t, picked, wide):
-            nc.vector.tensor_tensor(d_page[t][:].indirect(idx2[:]), picked[:], wide[:], ADD)
+        def scatter_d(t, picked):
+            nc.vector.tensor_tensor(d_page[t][:].indirect(idx2[:]), picked[:], ko_wide[:, t, :], ADD)
 
-        ko_wide = [spread_ko(t, "ko_wide%d" % t) for t in range(PACK)]
-        for t in range(3):
-            scatter_d(t, gather_xr(t, "picked%d" % t), ko_wide[t])
+        for t in range(2):
+            scatter_d(t, gather_xr(t, "picked%d" % t))
 
-        words = [sb.tile([P, 2, J], U32, name="words%d" % a, tag="words%d" % a, align_bytes=64) for a in range(PASSES)]
-        planes = sb.tile([P, 2, T], BF16, name="planes", tag="cast0", align_bytes=64)
-        nc.scalar.activation(planes[:], raw[0][:], COPY)
-        first = words[0][:, 0, :].bitcast(BF16).rearrange("p (j e) -> p j e", e=2)
-        for e in range(2):
-            nc.scalar.activation(first[:, :, e], planes[:, e, :].indirect(idx[:]), COPY)
-        for i in range(1, 2 * PASSES):
-            pairs = sb.tile([P, T, 2], BF16, name="pairs%d" % i, tag="cast%d" % i, align_bytes=64)
-            nc.scalar.activation(pairs[:], raw[i][:].rearrange("p e c -> p c e"), COPY)
+        woven0 = sb.tile([P, J, PACK], BF16, name="woven0", align_bytes=64)
+        words = sb.tile([P, 2, J], U32, name="words", align_bytes=64)
+
+        def cast_planes(u):
+            planes = sb.tile([P, 2, T], BF16, name="planes%d" % u, tag="cast%d" % u, align_bytes=64)
+            for e in range(2):
+                nc.scalar.activation(planes[:, e, :], raw[u][:, e, :], COPY)
+            return planes
+
+        def gather_on_scalar(u, planes):
+            for e in range(2):
+                nc.scalar.activation(woven0[:, :, 2 * u + e], planes[:, e, :].indirect(idx[:]), COPY)
+
+        def gather_on_vector(u):
+            pairs = sb.tile([P, T, 2], BF16, name="pairs%d" % u, align_bytes=64)
+            nc.scalar.activation(pairs[:], raw[2 + u][:].rearrange("p e c -> p c e"), COPY)
             window = pairs[:].rearrange("p c e -> p (c e)").bitcast(U32)
-            nc.vector.tensor_copy(words[i // 2][:, i % 2, :], window.indirect(idx[:]))
+            nc.vector.tensor_copy(words[:, u, :], window.indirect(idx[:]))
 
-        x_codes = {}
-        x_scales = {}
-
-        def quantise_x(a, first_block, blocks, tag):
-            width = blocks * P
-            entries = slice(first_block * P, first_block * P + width)
-            woven = sb.tile([P, width * PACK], BF16, name="woven%d_%d" % (a, first_block), tag=tag, align_bytes=64)
-            codes = sb.tile([P, width], U32, name="x_codes%d_%d" % (a, first_block), align_bytes=64)
-            scales = sb.tile([P, width], U8, name="x_scales%d_%d" % (a, first_block), align_bytes=64)
-            nc.scalar.copy(
-                woven[:].bitcast(U32).rearrange("p (j u) -> p j u", u=2), words[a][:, :, entries].rearrange("p u j -> p j u")
-            )
-            nc.vector.quantize_mx(out=codes[:].bitcast(FP8X4), scales=scales[:], in_=woven[:])
-            for b in range(blocks):
-                x_codes[a, first_block + b] = codes[:, b * P : (b + 1) * P]
-                x_scales[a, first_block + b] = scales[:, b * P : (b + 1) * P]
-
-        quantise_x(0, 0, 4, "raw3")
-        quantise_x(1, 0, 2, "woven_a")
-        quantise_x(1, 2, 2, "woven_b")
-        scatter_d(3, gather_xr(3, "woven_b"), ko_wide[3])
-
+        x_codes = [sb.tile([P, J], U32, name="x_codes%d" % a, align_bytes=64) for a in range(PASSES)]
+        x_scales = [sb.tile([P, J], U8, name="x_scales%d" % a, align_bytes=64) for a in range(PASSES)]
         acc = [ps.tile([P, N], F32, name="acc%d" % b) for b in range(J // P)]
-        for a in range(PASSES):
+
+        def quantise_and_multiply(a, woven, first):
+            nc.vector.quantize_mx(out=x_codes[a][:].bitcast(FP8X4), scales=x_scales[a][:], in_=woven)
             for b in range(J // P):
+                cols = slice(b * P, (b + 1) * P)
                 nc.tensor.matmul_mx(
                     out=acc[b][:],
-                    lhsT=x_codes[a, b].bitcast(FP8X4),
-                    lhsT_scale=x_scales[a, b],
+                    lhsT=x_codes[a][:, cols].bitcast(FP8X4),
+                    lhsT_scale=x_scales[a][:, cols],
                     rhs=w_words[:, a, :].bitcast(FP4X4),
                     rhs_scale=w_scales[:, a, :],
-                    start=(a == 0),
-                    stop=(a == PASSES - 1),
+                    start=first,
+                    stop=not first,
                 )
+
+        gather_on_scalar(0, cast_planes(0))
+        gather_on_vector(0)
+        gather_on_vector(1)
+        scatter_d(2, gather_xr(2, "picked2"))
+        last_planes = cast_planes(1)
+        woven1 = sb.tile([P, J * PACK], BF16, name="woven1", tag="raw1", align_bytes=64)
+        nc.scalar.copy(woven1[:].bitcast(U32).rearrange("p (j u) -> p j u", u=2), words[:].rearrange("p u j -> p j u"))
+        gather_on_scalar(1, last_planes)
+        quantise_and_multiply(1, woven1[:], True)
+        picked_last = gather_xr(3, "raw1")
+        quantise_and_multiply(0, woven0[:].rearrange("p j t -> p (j t)"), False)
+        scatter_d(3, picked_last)
+
         p_t = [sb.tile([P, PACK, P], F32, name="p_t%d" % b) for b in range(J // P)]
 
         def leave_bank(b):

@@ -37,15 +37,16 @@ def tile_list_copying_expert_pl_kernel(tc, xq, wa_words, wa_scales, xr, gb, ko, 
         gb_col = sb.tile([P, PACK], F32, name="gb_col")
         ko_col = sb.tile([P, PACK], F32, name="ko_col", tag="cast0", align_bytes=64)
         xr_sb = [sb.tile([P, T], F32, name="xr%d" % t) for t in range(PACK)]
-        raw = [sb.tile([P, 2, T], F32, name="raw%d" % i, tag="raw%d" % i, align_bytes=64) for i in range(2 * PASSES)]
+        raw_plane = [sb.tile([P, T], F32, name="raw_plane%d" % r, align_bytes=64) for r in range(PACK)]
+        raw_pair = [sb.tile([P, 2, T], F32, name="raw_pair%d" % u, align_bytes=64) for u in range(2)]
         w_words = sb.tile([P, PASSES, 2 * N], U8, name="w_words", align_bytes=64)
         w_scales = sb.tile([P, PASSES, N], U8, name="w_scales", align_bytes=64)
         ident = sb.tile([P, P], F32, name="ident")
-        d_page = [sb.tile([P, T], F32, name="d_page%d" % i) for i in range(PACK)]
+        d_page = {t: sb.tile([P, T], F32, name="d_page%d" % t) for t in (0, 1, 3)}
         p_page = [sb.tile([P, T], F32, name="p_page%d" % i) for i in range(2)]
 
         xr_rows = xr.rearrange("(p t) c -> p t c", t=PACK)
-        xq_rows = xq.rearrange("(a p u e) c -> a u p e c", a=PASSES, u=2, e=2)
+        xq_rows = xq.rearrange("(a p r) c -> a p r c", a=PASSES, r=PACK)
         y_rows = out_0.rearrange("(p t) c -> p t c", t=PACK)
 
         nc.scalar.dma_start(gb_col[:], gb.rearrange("o (p m) -> p (o m)", m=PACK))
@@ -53,21 +54,22 @@ def tile_list_copying_expert_pl_kernel(tc, xq, wa_words, wa_scales, xr, gb, ko, 
         nc.sync.dma_start(idx2[:], offs2)
         nc.sync.dma_start(xr_sb[0][:], xr_rows[:, 0, :])
         nc.sync.dma_start(idx[:], offs)
-        for e in range(2):
-            nc.sync.dma_start(raw[0][:, e, :], xq_rows[0, 0][:, e, :])
+        nc.sync.dma_start(raw_plane[0][:], xq_rows[0, :, 0, :])
         nc.sync.dma_start(xr_sb[1][:], xr_rows[:, 1, :])
-        nc.sync.dma_start(raw[2][:], xq_rows[1, 0])
-        nc.sync.dma_start(raw[3][:], xq_rows[1, 1])
-        nc.sync.dma_start(raw[1][:], xq_rows[0, 1])
+        nc.sync.dma_start(raw_plane[1][:], xq_rows[0, :, 1, :])
         nc.sync.dma_start(xr_sb[2][:], xr_rows[:, 2, :])
+        for u in range(2):
+            nc.sync.dma_start(raw_pair[u][:], xq_rows[1, :, 2 * u : 2 * u + 2, :])
+        for r in (2, 3):
+            nc.sync.dma_start(raw_plane[r][:], xq_rows[0, :, r, :])
         nc.sync.dma_start(w_words[:].bitcast(I32), wa_words.rearrange("a p c -> p a c").bitcast(I32))
         nc.sync.dma_start(xr_sb[3][:], xr_rows[:, 3, :])
 
         make_identity(nc, ident[:])
-        for page in d_page[:2]:
+        for page in (d_page[0], d_page[1]):
             nc.vector.memset(page[:], 0.0)
         nc.gpsimd.memset(w_scales[:].bitcast(I32), 0)
-        for page in d_page[2:] + p_page:
+        for page in (d_page[3], p_page[0], p_page[1]):
             nc.gpsimd.memset(page[:], 0.0)
         for q in range(4):
             nc.sync.dma_start(
@@ -82,36 +84,33 @@ def tile_list_copying_expert_pl_kernel(tc, xq, wa_words, wa_scales, xr, gb, ko, 
         nc.vector.tensor_scalar(
             gb_half[:].rearrange("p (n m) -> p n m", m=PACK), gb_ps[:].rearrange("p m n -> p n m"), 0.5, None, MULT
         )
-        ko_wide = sb.tile([P, PACK, J], F32, name="ko_wide")
-        nc.scalar.activation(ko_wide[:], ko_col[:].unsqueeze(2).to_broadcast([P, PACK, J]), COPY, scale=0.5)
+        ko_half = sb.tile([P, 1], F32, name="ko_half")
+        ko_wide = sb.tile([P, PACK - 1, J], F32, name="ko_wide")
+        nc.scalar.activation(ko_wide[:], ko_col[:, 0:3].unsqueeze(2).to_broadcast([P, PACK - 1, J]), COPY, scale=0.5)
+        nc.scalar.activation(ko_half[:], ko_col[:, 3:4], COPY, scale=0.5)
 
         def gather_xr(t, tag):
             picked = sb.tile([P, J], F32, name="picked%d" % t, tag=tag, align_bytes=64)
             nc.vector.tensor_tensor(picked[:], xr_sb[t][:].indirect(idx2[:]), gb_half[:], MULT)
             return picked
 
-        def scatter_d(t, picked):
-            nc.vector.tensor_tensor(d_page[t][:].indirect(idx2[:]), picked[:], ko_wide[:, t, :], ADD)
-
-        for t in range(2):
-            scatter_d(t, gather_xr(t, "picked%d" % t))
+        def scatter_d(t, picked, wide):
+            nc.vector.tensor_tensor(d_page[t][:].indirect(idx2[:]), picked[:], wide, ADD)
 
         woven0 = sb.tile([P, J, PACK], BF16, name="woven0", align_bytes=64)
         words = sb.tile([P, 2, J], U32, name="words", align_bytes=64)
 
-        def cast_planes(u):
-            planes = sb.tile([P, 2, T], BF16, name="planes%d" % u, tag="cast%d" % u, align_bytes=64)
-            for e in range(2):
-                nc.scalar.activation(planes[:, e, :], raw[u][:, e, :], COPY)
-            return planes
+        def cast_plane(r, tag):
+            plane = sb.tile([P, T], BF16, name="plane%d" % r, tag=tag, align_bytes=64)
+            nc.scalar.activation(plane[:], raw_plane[r][:], COPY)
+            return plane
 
-        def gather_on_scalar(u, planes):
-            for e in range(2):
-                nc.scalar.activation(woven0[:, :, 2 * u + e], planes[:, e, :].indirect(idx[:]), COPY)
+        def gather_plane(r, plane):
+            nc.scalar.activation(woven0[:, :, r], plane[:].indirect(idx[:]), COPY)
 
-        def gather_on_vector(u):
+        def gather_pair(u):
             pairs = sb.tile([P, T, 2], BF16, name="pairs%d" % u, align_bytes=64)
-            nc.scalar.activation(pairs[:], raw[2 + u][:].rearrange("p e c -> p c e"), COPY)
+            nc.scalar.activation(pairs[:], raw_pair[u][:].rearrange("p e c -> p c e"), COPY)
             window = pairs[:].rearrange("p c e -> p (c e)").bitcast(U32)
             nc.vector.tensor_copy(words[:, u, :], window.indirect(idx[:]))
 
@@ -133,18 +132,26 @@ def tile_list_copying_expert_pl_kernel(tc, xq, wa_words, wa_scales, xr, gb, ko, 
                     stop=not first,
                 )
 
-        gather_on_scalar(0, cast_planes(0))
-        gather_on_vector(0)
-        gather_on_vector(1)
-        scatter_d(2, gather_xr(2, "picked2"))
-        last_planes = cast_planes(1)
-        woven1 = sb.tile([P, J * PACK], BF16, name="woven1", tag="raw1", align_bytes=64)
+        scatter_d(0, gather_xr(0, "picked0"), ko_wide[:, 0, :])
+        for r in (0, 1):
+            gather_plane(r, cast_plane(r, "cast%d" % r))
+        scatter_d(1, gather_xr(1, "picked1"), ko_wide[:, 1, :])
+        picked2 = gather_xr(2, "picked2")
+        for u in range(2):
+            gather_pair(u)
+        d_page[2] = sb.tile([P, T], F32, name="d_page2", tag="raw_pair1", align_bytes=64)
+        nc.gpsimd.memset(d_page[2][:], 0.0)
+        scatter_d(2, picked2, ko_wide[:, 2, :])
+        gather_plane(2, cast_plane(2, "cast2"))
+        woven1 = sb.tile([P, J * PACK], BF16, name="woven1", align_bytes=64)
         nc.scalar.copy(woven1[:].bitcast(U32).rearrange("p (j u) -> p j u", u=2), words[:].rearrange("p u j -> p j u"))
-        gather_on_scalar(1, last_planes)
+        gather_plane(3, cast_plane(3, "words"))
+        picked3 = gather_xr(3, "picked3")
         quantise_and_multiply(1, woven1[:], True)
-        picked_last = gather_xr(3, "raw1")
         quantise_and_multiply(0, woven0[:].rearrange("p j t -> p (j t)"), False)
-        scatter_d(3, picked_last)
+        ko_last = sb.tile([P, J], F32, name="ko_last", tag="words", align_bytes=64)
+        nc.scalar.copy(ko_last[:], ko_half[:].to_broadcast([P, J]))
+        scatter_d(3, picked3, ko_last[:])
 
         p_t = [sb.tile([P, PACK, P], F32, name="p_t%d" % b) for b in range(J // P)]
 

@@ -17,12 +17,15 @@ FP4X4 = mybir.dt.float4_e2m1fn_x4
 MULT = mybir.AluOpType.mult
 ADD = mybir.AluOpType.add
 COPY = mybir.ActivationFunctionType.Copy
-IDENT = mybir.ActivationFunctionType.Identity
 
 P = 128
 PACK = 4
 PASSES = K // (P * PACK)
-HALF = T // 2
+QUADRANTS = 4
+GROUP = 16
+ALL_BLOCKS = [0, 1, 2, 3]
+HALF_BLOCKS = [[0, 1], [2, 3]]
+LAST = PACK - 1
 
 
 def tile_list_copying_expert_pl_kernel(tc, xq, wa_words, wa_scales, xr, gb, ko, offs, offs2, out_0, out_1, out_2):
@@ -32,46 +35,48 @@ def tile_list_copying_expert_pl_kernel(tc, xq, wa_words, wa_scales, xr, gb, ko, 
         sb = ctx.enter_context(tc.tile_pool(name="sb", bufs=1))
         ps = ctx.enter_context(tc.psum_pool(name="ps", bufs=1))
 
-        idx = lists.tile([P, J // 16], U16, name="idx")
-        idx2 = lists.tile([P, J // 16], U16, name="idx2")
+        idx = lists.tile([P, J // GROUP], U16, name="idx")
+        idx2 = lists.tile([P, J // GROUP], U16, name="idx2")
         gb_col = sb.tile([P, PACK], F32, name="gb_col")
-        ko_col = sb.tile([P, PACK], F32, name="ko_col", tag="cast0", align_bytes=64)
+        ko_col = sb.tile([P, PACK], F32, name="ko_col", align_bytes=64)
         xr_sb = [sb.tile([P, T], F32, name="xr%d" % t) for t in range(PACK)]
         raw_plane = [sb.tile([P, T], F32, name="raw_plane%d" % r, align_bytes=64) for r in range(PACK)]
         raw_pair = [sb.tile([P, 2, T], F32, name="raw_pair%d" % u, align_bytes=64) for u in range(2)]
         w_words = sb.tile([P, PASSES, 2 * N], U8, name="w_words", align_bytes=64)
         w_scales = sb.tile([P, PASSES, N], U8, name="w_scales", align_bytes=64)
         ident = sb.tile([P, P], F32, name="ident")
-        d_page = {t: sb.tile([P, T], F32, name="d_page%d" % t) for t in (0, 1, 3)}
+        d_page = {t: sb.tile([P, T], F32, name="d_page%d" % t) for t in (0, 1, LAST)}
         p_page = [sb.tile([P, T], F32, name="p_page%d" % i) for i in range(2)]
 
         xr_rows = xr.rearrange("(p t) c -> p t c", t=PACK)
         xq_rows = xq.rearrange("(a p r) c -> a p r c", a=PASSES, r=PACK)
         y_rows = out_0.rearrange("(p t) c -> p t c", t=PACK)
 
+        def list_columns(blocks):
+            return idx[:, blocks[0] * (P // GROUP) : (blocks[-1] + 1) * (P // GROUP)]
+
         nc.scalar.dma_start(gb_col[:], gb.rearrange("o (p m) -> p (o m)", m=PACK))
         nc.scalar.dma_start(ko_col[:], ko.rearrange("(p t) o -> p (t o)", t=PACK))
         nc.sync.dma_start(idx2[:], offs2)
         nc.sync.dma_start(xr_sb[0][:], xr_rows[:, 0, :])
         nc.sync.dma_start(idx[:], offs)
-        nc.sync.dma_start(raw_plane[0][:], xq_rows[0, :, 0, :])
-        nc.sync.dma_start(xr_sb[1][:], xr_rows[:, 1, :])
-        nc.sync.dma_start(raw_plane[1][:], xq_rows[0, :, 1, :])
-        nc.sync.dma_start(xr_sb[2][:], xr_rows[:, 2, :])
+        for r in (0, 1):
+            nc.sync.dma_start(raw_plane[r][:], xq_rows[0, :, r, :])
+            nc.sync.dma_start(xr_sb[r + 1][:], xr_rows[:, r + 1, :])
         for u in range(2):
             nc.sync.dma_start(raw_pair[u][:], xq_rows[1, :, 2 * u : 2 * u + 2, :])
-        for r in (2, 3):
+        for r in (2, LAST):
             nc.sync.dma_start(raw_plane[r][:], xq_rows[0, :, r, :])
         nc.sync.dma_start(w_words[:].bitcast(I32), wa_words.rearrange("a p c -> p a c").bitcast(I32))
-        nc.sync.dma_start(xr_sb[3][:], xr_rows[:, 3, :])
+        nc.sync.dma_start(xr_sb[LAST][:], xr_rows[:, LAST, :])
 
         make_identity(nc, ident[:])
         for page in (d_page[0], d_page[1]):
             nc.vector.memset(page[:], 0.0)
         nc.gpsimd.memset(w_scales[:].bitcast(I32), 0)
-        for page in (d_page[3], p_page[0], p_page[1]):
+        for page in (d_page[LAST], p_page[0], p_page[1]):
             nc.gpsimd.memset(page[:], 0.0)
-        for q in range(4):
+        for q in range(QUADRANTS):
             nc.sync.dma_start(
                 w_scales[32 * q : 32 * q + 4, :, :].bitcast(I32),
                 wa_scales[:, 4 * q : 4 * q + 4, :].rearrange("a r c -> r a c").bitcast(I32),
@@ -84,29 +89,27 @@ def tile_list_copying_expert_pl_kernel(tc, xq, wa_words, wa_scales, xr, gb, ko, 
         nc.vector.tensor_scalar(
             gb_half[:].rearrange("p (n m) -> p n m", m=PACK), gb_ps[:].rearrange("p m n -> p n m"), 0.5, None, MULT
         )
-        ko_half = sb.tile([P, 1], F32, name="ko_half")
-        ko_wide = sb.tile([P, PACK - 1, J], F32, name="ko_wide")
-        nc.scalar.activation(ko_wide[:], ko_col[:, 0:3].unsqueeze(2).to_broadcast([P, PACK - 1, J]), COPY, scale=0.5)
-        nc.scalar.activation(ko_half[:], ko_col[:, 3:4], COPY, scale=0.5)
+        ko_half_last = sb.tile([P, 1], F32, name="ko_half_last")
+        ko_wide = sb.tile([P, LAST, J], F32, name="ko_wide")
+        nc.scalar.activation(ko_wide[:], ko_col[:, 0:LAST].unsqueeze(2).to_broadcast([P, LAST, J]), COPY, scale=0.5)
+        nc.scalar.activation(ko_half_last[:], ko_col[:, LAST:PACK], COPY, scale=0.5)
 
         def gather_xr(t, tag):
             picked = sb.tile([P, J], F32, name="picked%d" % t, tag=tag, align_bytes=64)
             nc.vector.tensor_tensor(picked[:], xr_sb[t][:].indirect(idx2[:]), gb_half[:], MULT)
             return picked
 
-        def scatter_d(t, picked, wide):
-            nc.vector.tensor_tensor(d_page[t][:].indirect(idx2[:]), picked[:], wide, ADD)
+        def scatter_d(t, picked, ko_row):
+            nc.vector.tensor_tensor(d_page[t][:].indirect(idx2[:]), picked[:], ko_row, ADD)
 
-        woven0 = sb.tile([P, J, PACK], BF16, name="woven0", align_bytes=64)
+        woven0 = [sb.tile([P, J // 2, PACK], BF16, name="woven0_%d" % h, align_bytes=64) for h in range(2)]
         words = sb.tile([P, 2, J], U32, name="words", align_bytes=64)
 
-        def cast_plane(r, tag):
+        def gather_plane(r, tag):
             plane = sb.tile([P, T], BF16, name="plane%d" % r, tag=tag, align_bytes=64)
             nc.scalar.activation(plane[:], raw_plane[r][:], COPY)
-            return plane
-
-        def gather_plane(r, plane):
-            nc.scalar.activation(woven0[:, :, r], plane[:].indirect(idx[:]), COPY)
+            for h, blocks in enumerate(HALF_BLOCKS):
+                nc.scalar.activation(woven0[h][:, :, r], plane[:].indirect(list_columns(blocks)), COPY)
 
         def gather_pair(u):
             pairs = sb.tile([P, T, 2], BF16, name="pairs%d" % u, align_bytes=64)
@@ -114,27 +117,28 @@ def tile_list_copying_expert_pl_kernel(tc, xq, wa_words, wa_scales, xr, gb, ko, 
             window = pairs[:].rearrange("p c e -> p (c e)").bitcast(U32)
             nc.vector.tensor_copy(words[:, u, :], window.indirect(idx[:]))
 
-        x_codes = [sb.tile([P, J], U32, name="x_codes%d" % a, align_bytes=64) for a in range(PASSES)]
-        x_scales = [sb.tile([P, J], U8, name="x_scales%d" % a, align_bytes=64) for a in range(PASSES)]
-        acc = [ps.tile([P, N], F32, name="acc%d" % b) for b in range(J // P)]
+        acc = [ps.tile([P, N], F32, name="acc%d" % b) for b in ALL_BLOCKS]
 
-        def quantise_and_multiply(a, woven, first):
-            nc.vector.quantize_mx(out=x_codes[a][:].bitcast(FP8X4), scales=x_scales[a][:], in_=woven)
-            for b in range(J // P):
-                cols = slice(b * P, (b + 1) * P)
+        def quantise_and_multiply(a, blocks, woven, opens_sum):
+            width = len(blocks) * P
+            codes = sb.tile([P, width], U32, name="x_codes%d_%d" % (a, blocks[0]), align_bytes=64)
+            scales = sb.tile([P, width], U8, name="x_scales%d_%d" % (a, blocks[0]), align_bytes=64)
+            nc.vector.quantize_mx(out=codes[:].bitcast(FP8X4), scales=scales[:], in_=woven)
+            for i, b in enumerate(blocks):
+                cols = slice(i * P, (i + 1) * P)
                 nc.tensor.matmul_mx(
                     out=acc[b][:],
-                    lhsT=x_codes[a][:, cols].bitcast(FP8X4),
-                    lhsT_scale=x_scales[a][:, cols],
+                    lhsT=codes[:, cols].bitcast(FP8X4),
+                    lhsT_scale=scales[:, cols],
                     rhs=w_words[:, a, :].bitcast(FP4X4),
                     rhs_scale=w_scales[:, a, :],
-                    start=first,
-                    stop=not first,
+                    start=opens_sum,
+                    stop=not opens_sum,
                 )
 
         scatter_d(0, gather_xr(0, "picked0"), ko_wide[:, 0, :])
-        for r in (0, 1):
-            gather_plane(r, cast_plane(r, "cast%d" % r))
+        gather_plane(0, "ko_col")
+        gather_plane(1, "plane1")
         scatter_d(1, gather_xr(1, "picked1"), ko_wide[:, 1, :])
         picked2 = gather_xr(2, "picked2")
         for u in range(2):
@@ -142,79 +146,78 @@ def tile_list_copying_expert_pl_kernel(tc, xq, wa_words, wa_scales, xr, gb, ko, 
         d_page[2] = sb.tile([P, T], F32, name="d_page2", tag="raw_pair1", align_bytes=64)
         nc.gpsimd.memset(d_page[2][:], 0.0)
         scatter_d(2, picked2, ko_wide[:, 2, :])
-        gather_plane(2, cast_plane(2, "cast2"))
+        gather_plane(2, "plane2")
         woven1 = sb.tile([P, J * PACK], BF16, name="woven1", align_bytes=64)
         nc.scalar.copy(woven1[:].bitcast(U32).rearrange("p (j u) -> p j u", u=2), words[:].rearrange("p u j -> p j u"))
-        gather_plane(3, cast_plane(3, "words"))
-        picked3 = gather_xr(3, "picked3")
-        quantise_and_multiply(1, woven1[:], True)
-        quantise_and_multiply(0, woven0[:].rearrange("p j t -> p (j t)"), False)
-        ko_last = sb.tile([P, J], F32, name="ko_last", tag="words", align_bytes=64)
-        nc.scalar.copy(ko_last[:], ko_half[:].to_broadcast([P, J]))
-        scatter_d(3, picked3, ko_last[:])
+        gather_plane(LAST, "words")
+        quantise_and_multiply(1, ALL_BLOCKS, woven1[:], True)
+        picked_last = gather_xr(LAST, "woven1")
+        for h, blocks in enumerate(HALF_BLOCKS):
+            quantise_and_multiply(0, blocks, woven0[h][:].rearrange("p j t -> p (j t)"), False)
+        ko_wide_last = sb.tile([P, J], F32, name="ko_wide_last", tag="words", align_bytes=64)
+        nc.scalar.copy(ko_wide_last[:], ko_half_last[:].to_broadcast([P, J]))
+        scatter_d(LAST, picked_last, ko_wide_last[:])
 
-        p_t = [sb.tile([P, PACK, P], F32, name="p_t%d" % b) for b in range(J // P)]
-
-        def leave_bank(b):
+        p_t = [sb.tile([P, PACK, P], F32, name="p_t%d" % b) for b in ALL_BLOCKS]
+        for b in ALL_BLOCKS:
             nc.scalar.copy(p_t[b][:], acc[b][:].rearrange("p (q t) -> p t q", t=PACK))
+        p_slice = [sb.tile([P, J], F32, name="p_slice%d" % t) for t in range(PACK)]
+        for t in range(PACK):
+            turn = ps.tile([P, J], F32, name="turn%d" % t, tag="turn%d" % t)
+            for b in ALL_BLOCKS:
+                nc.tensor.transpose(turn[:, b * P : (b + 1) * P], p_t[b][:, t, :], ident[:])
+            nc.scalar.copy(p_slice[t][:], turn[:])
 
-        def turn_p(t, blocks, bank):
-            width = len(blocks) * P
-            turn = ps.tile([P, width], F32, name="turn%d_%d" % (t, blocks[0]), tag="turn%d" % bank)
-            for i, b in enumerate(blocks):
-                nc.tensor.transpose(turn[:, i * P : (i + 1) * P], p_t[b][:, t, :], ident[:])
-            p_sb = sb.tile([P, width], F32, name="p_sb%d_%d" % (t, blocks[0]))
-            nc.scalar.copy(p_sb[:], turn[:])
-            return p_sb
-
-        def scatter_p(t, blocks, p_sb):
-            entries = idx[:, blocks[0] * (P // 16) : (blocks[-1] + 1) * (P // 16)]
-            nc.vector.tensor_copy(p_page[t % 2][:].indirect(entries), p_sb[:])
-
-        leave_bank(0)
-        leave_bank(1)
-        scatter_p(0, [0, 1], turn_p(0, [0, 1], 0))
-        leave_bank(2)
-        leave_bank(3)
-        scatter_p(0, [2, 3], turn_p(0, [2, 3], 1))
-        p_rest = [turn_p(t, [0, 1, 2, 3], (t + 1) % 4) for t in range(1, PACK)]
+        def scatter_p(t):
+            nc.vector.tensor_copy(p_page[t % 2][:].indirect(idx[:]), p_slice[t][:])
 
         pieces = [slice(0, T // 4), slice(T // 4, 3 * T // 4), slice(3 * T // 4, T)]
         y_low = sb.tile([P, 2, T], F32, name="y_low")
         y_high = [sb.tile([P, 2, c.stop - c.start], F32, name="y_high%d" % i) for i, c in enumerate(pieces)]
-        y_bf = [sb.tile([P, c.stop - c.start, PACK], BF16, name="y_bf%d" % i, align_bytes=64) for i, c in enumerate(pieces)]
+        y_woven = [
+            sb.tile([P, c.stop - c.start, PACK], BF16, name="y_woven%d" % i, align_bytes=64) for i, c in enumerate(pieces)
+        ]
         y_codes = sb.tile([P, T], U32, name="y_codes", align_bytes=64)
         y_scales = sb.tile([P, T], U8, name="y_scales", align_bytes=64)
         codes_out = out_1[0].rearrange("p c r -> p (c r)").bitcast(I32)
 
         def add_low(t):
-            nc.gpsimd.tensor_tensor(y_low[:, t, :], p_page[t][:], d_page[t][:], ADD)
+            nc.gpsimd.tensor_tensor(y_low[:, t, :], p_page[t % 2][:], d_page[t][:], ADD)
             nc.sync.dma_start(y_rows[:, t, :], y_low[:, t, :])
 
         def add_high(engine, t):
             for i, cols in enumerate(pieces):
-                engine.tensor_tensor(y_high[i][:, t - 2, :], p_page[t - 2][:, cols], d_page[t][:, cols], ADD)
-                nc.sync.dma_start(y_rows[:, t, cols], y_high[i][:, t - 2, :])
+                engine.tensor_tensor(y_high[i][:, t % 2, :], p_page[t % 2][:, cols], d_page[t][:, cols], ADD)
+                nc.sync.dma_start(y_rows[:, t, cols], y_high[i][:, t % 2, :])
 
-        add_low(0)
-        scatter_p(1, [0, 1, 2, 3], p_rest[0])
-        add_low(1)
-        scatter_p(2, [0, 1, 2, 3], p_rest[1])
-        for i, cols in enumerate(pieces):
-            nc.scalar.activation(y_bf[i][:, :, 0:2], y_low[:, :, cols].rearrange("p e c -> p c e"), COPY)
-        add_high(nc.gpsimd, 2)
-        scatter_p(3, [0, 1, 2, 3], p_rest[2])
-        add_high(nc.vector, 3)
-        for i in (0, 2):
-            nc.scalar.activation(y_bf[i][:, :, 2:4], y_high[i][:].rearrange("p e c -> p c e"), COPY)
-        nc.vector.tensor_copy(y_bf[1][:, :, 2:4], y_high[1][:].rearrange("p e c -> p c e"))
-        for i, cols in enumerate(pieces):
+        def quantise_y(i):
+            cols = pieces[i]
             nc.vector.quantize_mx(
-                out=y_codes[:, cols].bitcast(FP8X4), scales=y_scales[:, cols], in_=y_bf[i][:].rearrange("p c t -> p (c t)")
+                out=y_codes[:, cols].bitcast(FP8X4),
+                scales=y_scales[:, cols],
+                in_=y_woven[i][:].rearrange("p c t -> p (c t)"),
             )
-            if i > 0:
-                done = slice(0, cols.stop) if i == 1 else cols
-                nc.sync.dma_start(codes_out[:, done], y_codes[:, done].bitcast(I32))
-        for q in range(4):
+
+        def store_codes(cols):
+            nc.sync.dma_start(codes_out[:, cols], y_codes[:, cols].bitcast(I32))
+
+        for t in (0, 1):
+            scatter_p(t)
+            add_low(t)
+        scatter_p(2)
+        for i, cols in enumerate(pieces):
+            nc.scalar.activation(y_woven[i][:, :, 0:2], y_low[:, :, cols].rearrange("p e c -> p c e"), COPY)
+        add_high(nc.gpsimd, 2)
+        scatter_p(LAST)
+        add_high(nc.vector, LAST)
+        for i in (0, 2):
+            nc.scalar.activation(y_woven[i][:, :, 2:4], y_high[i][:].rearrange("p e c -> p c e"), COPY)
+        nc.vector.tensor_copy(y_woven[1][:, :, 2:4], y_high[1][:].rearrange("p e c -> p c e"))
+        quantise_y(0)
+        quantise_y(1)
+        store_codes(slice(pieces[0].start, pieces[1].stop))
+        quantise_y(2)
+        store_codes(pieces[2])
+        for q in range(QUADRANTS):
             queue = nc.scalar if q % 2 == 0 else nc.sync
             queue.dma_start(out_2[0, 4 * q : 4 * q + 4, :].bitcast(I32), y_scales[32 * q : 32 * q + 4, :].bitcast(I32))

from contextlib import ExitStack

import concourse.mybir as mybir
from concourse.masks import make_identity

K, T, J, N = 1024, 1024, 512, 512
FLOPS = 2 * K * J * N

F32 = mybir.dt.float32
BF16 = mybir.dt.bfloat16
I32 = mybir.dt.int32
U32 = mybir.dt.uint32
U16 = mybir.dt.uint16
U8 = mybir.dt.uint8
FP8X4 = mybir.dt.float8_e4m3fn_x4
FP4X4 = mybir.dt.float4_e2m1fn_x4
MULT = mybir.AluOpType.mult
ADD = mybir.AluOpType.add
COPY = mybir.ActivationFunctionType.Copy

P = 128
PACK = 4
PASSES = K // (P * PACK)
QUADRANTS = 4
GROUP = 16
ALL_BLOCKS = [0, 1, 2, 3]
HALF_BLOCKS = [[0, 1], [2, 3]]
LAST = PACK - 1


def tile_list_copying_expert_pl_kernel(tc, xq, wa_words, wa_scales, xr, gb, ko, offs, offs2, out_0, out_1, out_2):
    nc = tc.nc
    with ExitStack() as ctx:
        lists = ctx.enter_context(tc.tile_pool(name="lists", bufs=1))
        sb = ctx.enter_context(tc.tile_pool(name="sb", bufs=1))
        ps = ctx.enter_context(tc.psum_pool(name="ps", bufs=1))

        idx = lists.tile([P, J // GROUP], U16, name="idx")
        idx2 = lists.tile([P, J // GROUP], U16, name="idx2")
        gb_col = sb.tile([P, PACK], F32, name="gb_col")
        ko_col = sb.tile([P, PACK], F32, name="ko_col", align_bytes=64)
        xr_sb = [sb.tile([P, T], F32, name="xr%d" % t) for t in range(PACK)]
        raw_plane = [sb.tile([P, T], F32, name="raw_plane%d" % r, align_bytes=64) for r in range(PACK)]
        raw_pair = [sb.tile([P, 2, T], F32, name="raw_pair%d" % u, align_bytes=64) for u in range(2)]
        w_words = sb.tile([P, PASSES, 2 * N], U8, name="w_words", align_bytes=64)
        w_scales = sb.tile([P, PASSES, N], U8, name="w_scales", align_bytes=64)
        ident = sb.tile([P, P], F32, name="ident")
        d_page = {t: sb.tile([P, T], F32, name="d_page%d" % t) for t in (0, 1, LAST)}
        p_page = [sb.tile([P, T], F32, name="p_page%d" % i) for i in range(2)]

        xr_rows = xr.rearrange("(p t) c -> p t c", t=PACK)
        xq_rows = xq.rearrange("(a p r) c -> a p r c", a=PASSES, r=PACK)
        y_rows = out_0.rearrange("(p t) c -> p t c", t=PACK)

        def list_columns(blocks):
            return idx[:, blocks[0] * (P // GROUP) : (blocks[-1] + 1) * (P // GROUP)]

        nc.scalar.dma_start(gb_col[:], gb.rearrange("o (p m) -> p (o m)", m=PACK))
        nc.scalar.dma_start(ko_col[:], ko.rearrange("(p t) o -> p (t o)", t=PACK))
        nc.sync.dma_start(idx2[:], offs2)
        nc.sync.dma_start(xr_sb[0][:], xr_rows[:, 0, :])
        nc.sync.dma_start(idx[:], offs)
        for r in (0, 1):
            nc.sync.dma_start(raw_plane[r][:], xq_rows[0, :, r, :])
            nc.sync.dma_start(xr_sb[r + 1][:], xr_rows[:, r + 1, :])
        for u in range(2):
            nc.sync.dma_start(raw_pair[u][:], xq_rows[1, :, 2 * u : 2 * u + 2, :])
        for r in (2, LAST):
            nc.sync.dma_start(raw_plane[r][:], xq_rows[0, :, r, :])
        nc.sync.dma_start(w_words[:].bitcast(I32), wa_words.rearrange("a p c -> p a c").bitcast(I32))
        nc.sync.dma_start(xr_sb[LAST][:], xr_rows[:, LAST, :])

        make_identity(nc, ident[:])
        for page in (d_page[0], d_page[1]):
            nc.vector.memset(page[:], 0.0)
        nc.gpsimd.memset(w_scales[:].bitcast(I32), 0)
        for page in (d_page[LAST], p_page[0], p_page[1]):
            nc.gpsimd.memset(page[:], 0.0)
        for q in range(QUADRANTS):
            nc.sync.dma_start(
                w_scales[32 * q : 32 * q + 4, :, :].bitcast(I32),
                wa_scales[:, 4 * q : 4 * q + 4, :].rearrange("a r c -> r a c").bitcast(I32),
            )

        gb_ps = ps.tile([P, PACK, P], F32, name="gb_ps", tag="turn0")
        for m in range(PACK):
            nc.tensor.transpose(gb_ps[:, m, :], gb_col[:, m : m + 1].to_broadcast([P, P]), ident[:])
        gb_half = sb.tile([P, J], F32, name="gb_half")
        nc.vector.tensor_scalar(
            gb_half[:].rearrange("p (n m) -> p n m", m=PACK), gb_ps[:].rearrange("p m n -> p n m"), 0.5, None, MULT
        )
        ko_half_last = sb.tile([P, 1], F32, name="ko_half_last")
        ko_wide = sb.tile([P, LAST, J], F32, name="ko_wide")
        nc.scalar.activation(ko_wide[:], ko_col[:, 0:LAST].unsqueeze(2).to_broadcast([P, LAST, J]), COPY, scale=0.5)
        nc.scalar.activation(ko_half_last[:], ko_col[:, LAST:PACK], COPY, scale=0.5)

        def gather_xr(t, tag):
            picked = sb.tile([P, J], F32, name="picked%d" % t, tag=tag, align_bytes=64)
            nc.vector.tensor_tensor(picked[:], xr_sb[t][:].indirect(idx2[:]), gb_half[:], MULT)
            return picked

        def scatter_d(t, picked, ko_row):
            nc.vector.tensor_tensor(d_page[t][:].indirect(idx2[:]), picked[:], ko_row, ADD)

        woven0 = [sb.tile([P, J // 2, PACK], BF16, name="woven0_%d" % h, align_bytes=64) for h in range(2)]
        words = sb.tile([P, 2, J], U32, name="words", align_bytes=64)

        def gather_plane(r, tag):
            plane = sb.tile([P, T], BF16, name="plane%d" % r, tag=tag, align_bytes=64)
            nc.scalar.activation(plane[:], raw_plane[r][:], COPY)
            for h, blocks in enumerate(HALF_BLOCKS):
                nc.scalar.activation(woven0[h][:, :, r], plane[:].indirect(list_columns(blocks)), COPY)

        def gather_pair(u):
            pairs = sb.tile([P, T, 2], BF16, name="pairs%d" % u, align_bytes=64)
            nc.scalar.activation(pairs[:], raw_pair[u][:].rearrange("p e c -> p c e"), COPY)
            window = pairs[:].rearrange("p c e -> p (c e)").bitcast(U32)
            nc.vector.tensor_copy(words[:, u, :], window.indirect(idx[:]))

        acc = [ps.tile([P, N], F32, name="acc%d" % b) for b in ALL_BLOCKS]

        def quantise_and_multiply(a, blocks, woven, opens_sum):
            width = len(blocks) * P
            codes = sb.tile([P, width], U32, name="x_codes%d_%d" % (a, blocks[0]), align_bytes=64)
            scales = sb.tile([P, width], U8, name="x_scales%d_%d" % (a, blocks[0]), align_bytes=64)
            nc.vector.quantize_mx(out=codes[:].bitcast(FP8X4), scales=scales[:], in_=woven)
            for i, b in enumerate(blocks):
                cols = slice(i * P, (i + 1) * P)
                nc.tensor.matmul_mx(
                    out=acc[b][:],
                    lhsT=codes[:, cols].bitcast(FP8X4),
                    lhsT_scale=scales[:, cols],
                    rhs=w_words[:, a, :].bitcast(FP4X4),
                    rhs_scale=w_scales[:, a, :],
                    start=opens_sum,
                    stop=not opens_sum,
                )

        scatter_d(0, gather_xr(0, "picked0"), ko_wide[:, 0, :])
        gather_plane(0, "ko_col")
        gather_plane(1, "plane1")
        scatter_d(1, gather_xr(1, "picked1"), ko_wide[:, 1, :])
        picked2 = gather_xr(2, "picked2")
        for u in range(2):
            gather_pair(u)
        d_page[2] = sb.tile([P, T], F32, name="d_page2", tag="raw_pair1", align_bytes=64)
        nc.gpsimd.memset(d_page[2][:], 0.0)
        scatter_d(2, picked2, ko_wide[:, 2, :])
        gather_plane(2, "plane2")
        woven1 = sb.tile([P, J * PACK], BF16, name="woven1", align_bytes=64)
        nc.scalar.copy(woven1[:].bitcast(U32).rearrange("p (j u) -> p j u", u=2), words[:].rearrange("p u j -> p j u"))
        gather_plane(LAST, "words")
        quantise_and_multiply(1, ALL_BLOCKS, woven1[:], True)
        picked_last = gather_xr(LAST, "woven1")
        for h, blocks in enumerate(HALF_BLOCKS):
            quantise_and_multiply(0, blocks, woven0[h][:].rearrange("p j t -> p (j t)"), False)
        ko_wide_last = sb.tile([P, J], F32, name="ko_wide_last", tag="words", align_bytes=64)
        nc.scalar.copy(ko_wide_last[:], ko_half_last[:].to_broadcast([P, J]))
        scatter_d(LAST, picked_last, ko_wide_last[:])

        p_t = [sb.tile([P, PACK, P], F32, name="p_t%d" % b) for b in ALL_BLOCKS]
        for b in ALL_BLOCKS:
            nc.scalar.copy(p_t[b][:], acc[b][:].rearrange("p (q t) -> p t q", t=PACK))
        p_slice = [sb.tile([P, J], F32, name="p_slice%d" % t) for t in range(PACK)]
        for t in range(PACK):
            turn = ps.tile([P, J], F32, name="turn%d" % t, tag="turn%d" % t)
            for b in ALL_BLOCKS:
                nc.tensor.transpose(turn[:, b * P : (b + 1) * P], p_t[b][:, t, :], ident[:])
            nc.scalar.copy(p_slice[t][:], turn[:])

        def scatter_p(t):
            nc.vector.tensor_copy(p_page[t % 2][:].indirect(idx[:]), p_slice[t][:])

        pieces = [slice(0, T // 4), slice(T // 4, 3 * T // 4), slice(3 * T // 4, T)]
        y_low = sb.tile([P, 2, T], F32, name="y_low")
        y_high = [sb.tile([P, 2, c.stop - c.start], F32, name="y_high%d" % i) for i, c in enumerate(pieces)]
        y_woven = [
            sb.tile([P, c.stop - c.start, PACK], BF16, name="y_woven%d" % i, align_bytes=64) for i, c in enumerate(pieces)
        ]
        y_codes = sb.tile([P, T], U32, name="y_codes", align_bytes=64)
        y_scales = sb.tile([P, T], U8, name="y_scales", align_bytes=64)
        codes_out = out_1[0].rearrange("p c r -> p (c r)").bitcast(I32)

        def add_low(t):
            nc.gpsimd.tensor_tensor(y_low[:, t, :], p_page[t % 2][:], d_page[t][:], ADD)
            nc.sync.dma_start(y_rows[:, t, :], y_low[:, t, :])

        def add_high(engine, t):
            for i, cols in enumerate(pieces):
                engine.tensor_tensor(y_high[i][:, t % 2, :], p_page[t % 2][:, cols], d_page[t][:, cols], ADD)
                nc.sync.dma_start(y_rows[:, t, cols], y_high[i][:, t % 2, :])

        def quantise_y(i):
            cols = pieces[i]
            nc.vector.quantize_mx(
                out=y_codes[:, cols].bitcast(FP8X4),
                scales=y_scales[:, cols],
                in_=y_woven[i][:].rearrange("p c t -> p (c t)"),
            )

        def store_codes(cols):
            nc.sync.dma_start(codes_out[:, cols], y_codes[:, cols].bitcast(I32))

        for t in (0, 1):
            scatter_p(t)
            add_low(t)
        scatter_p(2)
        for i, cols in enumerate(pieces):
            nc.scalar.activation(y_woven[i][:, :, 0:2], y_low[:, :, cols].rearrange("p e c -> p c e"), COPY)
        add_high(nc.gpsimd, 2)
        scatter_p(LAST)
        add_high(nc.vector, LAST)
        for i in (0, 2):
            nc.scalar.activation(y_woven[i][:, :, 2:4], y_high[i][:].rearrange("p e c -> p c e"), COPY)
        nc.vector.tensor_copy(y_woven[1][:, :, 2:4], y_high[1][:].rearrange("p e c -> p c e"))
        quantise_y(0)
        quantise_y(1)
        store_codes(slice(pieces[0].start, pieces[1].stop))
        quantise_y(2)
        store_codes(pieces[2])
        for q in range(QUADRANTS):
            queue = nc.scalar if q % 2 == 0 else nc.sync
            queue.dma_start(out_2[0, 4 * q : 4 * q + 4, :].bitcast(I32), y_scales[32 * q : 32 * q + 4, :].bitcast(I32))
